import numpy as np
import ml_dtypes

BF16 = ml_dtypes.bfloat16


def bf(x):
    return np.asarray(x, np.float32).astype(BF16)


def f32(x):
    return np.asarray(x, np.float32)


def f64(x):
    return np.asarray(x).astype(np.float64)


def striped(idx):
    return np.tile(idx.reshape(-1, 16).T, (8, 1))


S, K, M, N, B, Q = 512, 512, 256, 192, 2, 96


def setup_inputs():
    return {"base": bf(np.random.standard_normal((B, M, S))), "x": bf(np.random.standard_normal((K, N))), "w": bf(np.random.standard_normal((K, M)) / np.sqrt(K)), "b": f32(0.5 * np.random.standard_normal((M, 1))), "offs": striped(np.random.permutation(S)[:N])}


def reference(base, x, w, b, offs):
    idx = offs[:16].T.reshape(-1)
    z = f64(base).copy()
    for i in range(B):
        z[i][:, idx[i * Q : (i + 1) * Q]] += f64(w).T @ f64(x)[:, i * Q : (i + 1) * Q]
    return z + f64(b)

@@ -1,0 +1,76 @@
+import concourse.mybir as mybir
+from concourse.masks import make_identity
+
+BF16, F32, U16 = mybir.dt.bfloat16, mybir.dt.float32, mybir.dt.uint16
+
+P = 128
+SEQS = 2
+TOKENS = 512
+K = 512
+M = 256
+N = 192
+PIECE = N // SEQS
+K_BLOCKS = K // P
+M_BLOCKS = M // P
+PIECE_COLS = PIECE // 16
+
+FLOPS = 2 * K * M * N
+
+
+def tile_scatter_matmul_kernel(tc, base, x, w, b, offs, out):
+    nc = tc.nc
+    with (
+        tc.tile_pool(name="held", bufs=1) as held,
+        tc.psum_pool(name="windows", bufs=1) as windows,
+    ):
+        offsets = held.tile([P, N // 16], U16, name="offsets")
+        nc.sync.dma_start(offsets[:], offs)
+
+        ident = held.tile([P, P], BF16, name="ident")
+        make_identity(nc, ident[:])
+
+        blocks = [(i, mb) for i in range(SEQS) for mb in range(M_BLOCKS)]
+
+        base_sb = {}
+        for n, (i, mb) in enumerate(blocks):
+            base_sb[(i, mb)] = held.tile([P, TOKENS], BF16, name="base_%d_%d" % (i, mb))
+            queue = nc.sync if n % 2 == 0 else nc.scalar
+            queue.dma_start(base_sb[(i, mb)][:], base[i, mb * P : (mb + 1) * P, :])
+
+        w_sb = held.tile([P, K_BLOCKS, M], BF16, name="w_sb")
+        nc.sync.dma_start(w_sb[:], w.rearrange("(kb p) m -> p kb m", p=P))
+        x_sb = held.tile([P, K_BLOCKS, N], BF16, name="x_sb")
+        nc.scalar.dma_start(x_sb[:], x.rearrange("(kb p) n -> p kb n", p=P))
+
+        bias = held.tile([P, M_BLOCKS], F32, name="bias")
+        nc.gpsimd.dma_start(bias[:], b.rearrange("(mb p) o -> p (mb o)", p=P))
+
+        window = {}
+        for i, mb in blocks:
+            window[(i, mb)] = windows.tile([P, TOKENS], F32, name="window_%d_%d" % (i, mb))
+            nc.tensor.matmul(window[(i, mb)][:], ident[:], base_sb[(i, mb)][:], start=True, stop=False)
+
+        for n, (i, mb) in enumerate(blocks):
+            piece = offsets[:, i * PIECE_COLS : (i + 1) * PIECE_COLS]
+            for kb in range(K_BLOCKS):
+                nc.tensor.matmul(
+                    window[(i, mb)][:].indirect(piece),
+                    w_sb[:, kb, mb * P : (mb + 1) * P],
+                    x_sb[:, kb, i * PIECE : (i + 1) * PIECE],
+                    start=False,
+                    stop=(kb == K_BLOCKS - 1),
+                )
+            result = held.tile([P, TOKENS], F32, name="result_%d_%d" % (i, mb))
+            if n % 2 == 0:
+                nc.vector.tensor_scalar(
+                    result[:], window[(i, mb)][:], bias[:, mb : mb + 1], None, mybir.AluOpType.add
+                )
+                nc.sync.dma_start(out[i, mb * P : (mb + 1) * P, :], result[:])
+            else:
+                nc.scalar.activation(
+                    result[:],
+                    window[(i, mb)][:],
+                    mybir.ActivationFunctionType.Identity,
+                    bias=bias[:, mb : mb + 1],
+                )
+                nc.scalar.dma_start(out[i, mb * P : (mb + 1) * P, :], result[:])

@@ -13,6 +13,8 @@ PIECE = N // SEQS
 K_BLOCKS = K // P
 M_BLOCKS = M // P
 PIECE_COLS = PIECE // 16
+WARM_COLS = 256
+WARM_UP = 6
 
 FLOPS = 2 * K * M * N
 
@@ -23,13 +25,10 @@ def tile_scatter_matmul_kernel(tc, base, x, w, b, offs, out):
         tc.tile_pool(name="held", bufs=1) as held,
         tc.psum_pool(name="windows", bufs=1) as windows,
     ):
-        offsets = held.tile([P, N // 16], U16, name="offsets")
-        nc.sync.dma_start(offsets[:], offs)
-
-        ident = held.tile([P, P], BF16, name="ident")
-        make_identity(nc, ident[:])
-
         blocks = [(i, mb) for i in range(SEQS) for mb in range(M_BLOCKS)]
+
+        bias = held.tile([P, M_BLOCKS], F32, name="bias")
+        nc.scalar.dma_start(bias[:], b.rearrange("(mb p) o -> p (mb o)", p=P))
 
         base_sb = {}
         for n, (i, mb) in enumerate(blocks):
@@ -37,13 +36,22 @@ def tile_scatter_matmul_kernel(tc, base, x, w, b, offs, out):
             queue = nc.sync if n % 2 == 0 else nc.scalar
             queue.dma_start(base_sb[(i, mb)][:], base[i, mb * P : (mb + 1) * P, :])
 
+        offsets = held.tile([P, N // 16], U16, name="offsets")
+        nc.sync.dma_start(offsets[:], offs)
+
         w_sb = held.tile([P, K_BLOCKS, M], BF16, name="w_sb")
         nc.sync.dma_start(w_sb[:], w.rearrange("(kb p) m -> p kb m", p=P))
         x_sb = held.tile([P, K_BLOCKS, N], BF16, name="x_sb")
         nc.scalar.dma_start(x_sb[:], x.rearrange("(kb p) n -> p kb n", p=P))
 
-        bias = held.tile([P, M_BLOCKS], F32, name="bias")
-        nc.gpsimd.dma_start(bias[:], b.rearrange("(mb p) o -> p (mb o)", p=P))
+        zeros = held.tile([P, WARM_COLS], BF16, name="zeros")
+        nc.vector.memset(zeros[:], 0.0)
+        unread = windows.tile([P, WARM_COLS], F32, name="unread")
+        for n in range(WARM_UP):
+            nc.tensor.matmul(unread[:], zeros[:, 0:P], zeros[:], start=True, stop=True)
+
+        ident = held.tile([P, P], BF16, name="ident")
+        make_identity(nc, ident[:])
 
         window = {}
         for i, mb in blocks:

@@ -13,6 +13,7 @@ PIECE = N // SEQS
 K_BLOCKS = K // P
 M_BLOCKS = M // P
 PIECE_COLS = PIECE // 16
+HALF = TOKENS // 2
 WARM_COLS = 256
 WARM_UP = 6
 
@@ -40,9 +41,9 @@ def tile_scatter_matmul_kernel(tc, base, x, w, b, offs, out):
         nc.sync.dma_start(offsets[:], offs)
 
         w_sb = held.tile([P, K_BLOCKS, M], BF16, name="w_sb")
-        nc.sync.dma_start(w_sb[:], w.rearrange("(kb p) m -> p kb m", p=P))
+        nc.sync.dma_start(w_sb[:], w.rearrange("(p kb) m -> p kb m", p=P))
         x_sb = held.tile([P, K_BLOCKS, N], BF16, name="x_sb")
-        nc.scalar.dma_start(x_sb[:], x.rearrange("(kb p) n -> p kb n", p=P))
+        nc.scalar.dma_start(x_sb[:], x.rearrange("(p kb) n -> p kb n", p=P))
 
         zeros = held.tile([P, WARM_COLS], BF16, name="zeros")
         nc.vector.memset(zeros[:], 0.0)
@@ -69,16 +70,21 @@ def tile_scatter_matmul_kernel(tc, base, x, w, b, offs, out):
                     stop=(kb == K_BLOCKS - 1),
                 )
             result = held.tile([P, TOKENS], F32, name="result_%d_%d" % (i, mb))
-            if n % 2 == 0:
-                nc.vector.tensor_scalar(
-                    result[:], window[(i, mb)][:], bias[:, mb : mb + 1], None, mybir.AluOpType.add
-                )
-                nc.sync.dma_start(out[i, mb * P : (mb + 1) * P, :], result[:])
-            else:
-                nc.scalar.activation(
-                    result[:],
-                    window[(i, mb)][:],
-                    mybir.ActivationFunctionType.Identity,
-                    bias=bias[:, mb : mb + 1],
-                )
-                nc.scalar.dma_start(out[i, mb * P : (mb + 1) * P, :], result[:])
+            for lo in range(0, TOKENS, HALF):
+                if n % 2 == 0:
+                    nc.vector.tensor_scalar(
+                        result[:, lo : lo + HALF],
+                        window[(i, mb)][:, lo : lo + HALF],
+                        bias[:, mb : mb + 1],
+                        None,
+                        mybir.AluOpType.add,
+                    )
+                    nc.sync.dma_start(out[i, mb * P : (mb + 1) * P, lo : lo + HALF], result[:, lo : lo + HALF])
+                else:
+                    nc.scalar.activation(
+                        result[:, lo : lo + HALF],
+                        window[(i, mb)][:, lo : lo + HALF],
+                        mybir.ActivationFunctionType.Identity,
+                        bias=bias[:, mb : mb + 1],
+                    )
+                    nc.scalar.dma_start(out[i, mb * P : (mb + 1) * P, lo : lo + HALF], result[:, lo : lo + HALF])

@@ -29,7 +29,7 @@ def tile_scatter_matmul_kernel(tc, base, x, w, b, offs, out):
         blocks = [(i, mb) for i in range(SEQS) for mb in range(M_BLOCKS)]
 
         bias = held.tile([P, M_BLOCKS], F32, name="bias")
-        nc.scalar.dma_start(bias[:], b.rearrange("(mb p) o -> p (mb o)", p=P))
+        nc.gpsimd.dma_start(bias[:], b.rearrange("(mb p) o -> p (mb o)", p=P))
 
         base_sb = {}
         for n, (i, mb) in enumerate(blocks):
@@ -70,21 +70,12 @@ def tile_scatter_matmul_kernel(tc, base, x, w, b, offs, out):
                     stop=(kb == K_BLOCKS - 1),
                 )
             result = held.tile([P, TOKENS], F32, name="result_%d_%d" % (i, mb))
-            for lo in range(0, TOKENS, HALF):
-                if n % 2 == 0:
-                    nc.vector.tensor_scalar(
-                        result[:, lo : lo + HALF],
-                        window[(i, mb)][:, lo : lo + HALF],
-                        bias[:, mb : mb + 1],
-                        None,
-                        mybir.AluOpType.add,
-                    )
-                    nc.sync.dma_start(out[i, mb * P : (mb + 1) * P, lo : lo + HALF], result[:, lo : lo + HALF])
-                else:
-                    nc.scalar.activation(
-                        result[:, lo : lo + HALF],
-                        window[(i, mb)][:, lo : lo + HALF],
-                        mybir.ActivationFunctionType.Identity,
-                        bias=bias[:, mb : mb + 1],
-                    )
-                    nc.scalar.dma_start(out[i, mb * P : (mb + 1) * P, lo : lo + HALF], result[:, lo : lo + HALF])
+            for queue, lo in ((nc.sync, 0), (nc.scalar, HALF)):
+                nc.vector.tensor_scalar(
+                    result[:, lo : lo + HALF],
+                    window[(i, mb)][:, lo : lo + HALF],
+                    bias[:, mb : mb + 1],
+                    None,
+                    mybir.AluOpType.add,
+                )
+                queue.dma_start(out[i, mb * P : (mb + 1) * P, lo : lo + HALF], result[:, lo : lo + HALF])

@@ -29,7 +29,6 @@ def tile_scatter_matmul_kernel(tc, base, x, w, b, offs, out):
         blocks = [(i, mb) for i in range(SEQS) for mb in range(M_BLOCKS)]
 
         bias = held.tile([P, M_BLOCKS], F32, name="bias")
-        nc.gpsimd.dma_start(bias[:], b.rearrange("(mb p) o -> p (mb o)", p=P))
 
         base_sb = {}
         for n, (i, mb) in enumerate(blocks):
@@ -44,6 +43,8 @@ def tile_scatter_matmul_kernel(tc, base, x, w, b, offs, out):
         nc.sync.dma_start(w_sb[:], w.rearrange("(p kb) m -> p kb m", p=P))
         x_sb = held.tile([P, K_BLOCKS, N], BF16, name="x_sb")
         nc.scalar.dma_start(x_sb[:], x.rearrange("(p kb) n -> p kb n", p=P))
+
+        nc.scalar.dma_start(bias[:], b.rearrange("(mb p) o -> p (mb o)", p=P))
 
         zeros = held.tile([P, WARM_COLS], BF16, name="zeros")
         nc.vector.memset(zeros[:], 0.0)

@@ -26,6 +26,9 @@ def tile_scatter_matmul_kernel(tc, base, x, w, b, offs, out):
         tc.tile_pool(name="held", bufs=1) as held,
         tc.psum_pool(name="windows", bufs=1) as windows,
     ):
+        zeros = held.tile([P, WARM_COLS], BF16, name="zeros")
+        nc.gpsimd.memset(zeros[:], 0.0)
+
         blocks = [(i, mb) for i in range(SEQS) for mb in range(M_BLOCKS)]
 
         bias = held.tile([P, M_BLOCKS], F32, name="bias")
@@ -46,8 +49,6 @@ def tile_scatter_matmul_kernel(tc, base, x, w, b, offs, out):
 
         nc.scalar.dma_start(bias[:], b.rearrange("(mb p) o -> p (mb o)", p=P))
 
-        zeros = held.tile([P, WARM_COLS], BF16, name="zeros")
-        nc.vector.memset(zeros[:], 0.0)
         unread = windows.tile([P, WARM_COLS], F32, name="unread")
         for n in range(WARM_UP):
             nc.tensor.matmul(unread[:], zeros[:, 0:P], zeros[:], start=True, stop=True)

@@ -36,8 +36,7 @@ def tile_scatter_matmul_kernel(tc, base, x, w, b, offs, out):
         base_sb = {}
         for n, (i, mb) in enumerate(blocks):
             base_sb[(i, mb)] = held.tile([P, TOKENS], BF16, name="base_%d_%d" % (i, mb))
-            queue = nc.sync if n % 2 == 0 else nc.scalar
-            queue.dma_start(base_sb[(i, mb)][:], base[i, mb * P : (mb + 1) * P, :])
+            nc.sync.dma_start(base_sb[(i, mb)][:], base[i, mb * P : (mb + 1) * P, :])
 
         offsets = held.tile([P, N // 16], U16, name="offsets")
         nc.sync.dma_start(offsets[:], offs)
@@ -45,9 +44,9 @@ def tile_scatter_matmul_kernel(tc, base, x, w, b, offs, out):
         w_sb = held.tile([P, K_BLOCKS, M], BF16, name="w_sb")
         nc.sync.dma_start(w_sb[:], w.rearrange("(p kb) m -> p kb m", p=P))
         x_sb = held.tile([P, K_BLOCKS, N], BF16, name="x_sb")
-        nc.scalar.dma_start(x_sb[:], x.rearrange("(p kb) n -> p kb n", p=P))
+        nc.sync.dma_start(x_sb[:], x.rearrange("(p kb) n -> p kb n", p=P))
 
-        nc.scalar.dma_start(bias[:], b.rearrange("(mb p) o -> p (mb o)", p=P))
+        nc.sync.dma_start(bias[:], b.rearrange("(mb p) o -> p (mb o)", p=P))
 
         unread = windows.tile([P, WARM_COLS], F32, name="unread")
         for n in range(WARM_UP):

@@ -71,7 +71,7 @@ def tile_scatter_matmul_kernel(tc, base, x, w, b, offs, out):
                     stop=(kb == K_BLOCKS - 1),
                 )
             result = held.tile([P, TOKENS], F32, name="result_%d_%d" % (i, mb))
-            for queue, lo in ((nc.sync, 0), (nc.scalar, HALF)):
+            for lo in (0, HALF):
                 nc.vector.tensor_scalar(
                     result[:, lo : lo + HALF],
                     window[(i, mb)][:, lo : lo + HALF],
@@ -79,4 +79,4 @@ def tile_scatter_matmul_kernel(tc, base, x, w, b, offs, out):
                     None,
                     mybir.AluOpType.add,
                 )
-                queue.dma_start(out[i, mb * P : (mb + 1) * P, lo : lo + HALF], result[:, lo : lo + HALF])
+                nc.sync.dma_start(out[i, mb * P : (mb + 1) * P, lo : lo + HALF], result[:, lo : lo + HALF])

@@ -34,9 +34,9 @@ def tile_scatter_matmul_kernel(tc, base, x, w, b, offs, out):
         bias = held.tile([P, M_BLOCKS], F32, name="bias")
 
         base_sb = {}
-        for n, (i, mb) in enumerate(blocks):
-            base_sb[(i, mb)] = held.tile([P, TOKENS], BF16, name="base_%d_%d" % (i, mb))
-            nc.sync.dma_start(base_sb[(i, mb)][:], base[i, mb * P : (mb + 1) * P, :])
+        for i in range(SEQS):
+            base_sb[i] = held.tile([P, M_BLOCKS, TOKENS], BF16, name="base_%d" % i)
+            nc.sync.dma_start(base_sb[i][:], base[i].rearrange("(mb p) t -> p mb t", p=P))
 
         offsets = held.tile([P, N // 16], U16, name="offsets")
         nc.sync.dma_start(offsets[:], offs)
@@ -58,7 +58,7 @@ def tile_scatter_matmul_kernel(tc, base, x, w, b, offs, out):
         window = {}
         for i, mb in blocks:
             window[(i, mb)] = windows.tile([P, TOKENS], F32, name="window_%d_%d" % (i, mb))
-            nc.tensor.matmul(window[(i, mb)][:], ident[:], base_sb[(i, mb)][:], start=True, stop=False)
+            nc.tensor.matmul(window[(i, mb)][:], ident[:], base_sb[i][:, mb, :], start=True, stop=False)
 
         for n, (i, mb) in enumerate(blocks):
             piece = offsets[:, i * PIECE_COLS : (i + 1) * PIECE_COLS]

@@ -11,6 +11,7 @@ M = 256
 N = 192
 PIECE = N // SEQS
 K_BLOCKS = K // P
+K_HALF = K_BLOCKS // 2
 M_BLOCKS = M // P
 PIECE_COLS = PIECE // 16
 HALF = TOKENS // 2
@@ -41,10 +42,14 @@ def tile_scatter_matmul_kernel(tc, base, x, w, b, offs, out):
         offsets = held.tile([P, N // 16], U16, name="offsets")
         nc.sync.dma_start(offsets[:], offs)
 
-        w_sb = held.tile([P, K_BLOCKS, M], BF16, name="w_sb")
-        nc.sync.dma_start(w_sb[:], w.rearrange("(p kb) m -> p kb m", p=P))
-        x_sb = held.tile([P, K_BLOCKS, N], BF16, name="x_sb")
-        nc.sync.dma_start(x_sb[:], x.rearrange("(p kb) n -> p kb n", p=P))
+        w_rows = w.rearrange("(p kb) m -> p kb m", p=P)
+        x_rows = x.rearrange("(p kb) n -> p kb n", p=P)
+        w_sb, x_sb = [], []
+        for h in range(K_BLOCKS // K_HALF):
+            w_sb.append(held.tile([P, K_HALF, M], BF16, name="w_%d" % h))
+            nc.sync.dma_start(w_sb[h][:], w_rows[:, h * K_HALF : (h + 1) * K_HALF, :])
+            x_sb.append(held.tile([P, K_HALF, N], BF16, name="x_%d" % h))
+            nc.sync.dma_start(x_sb[h][:], x_rows[:, h * K_HALF : (h + 1) * K_HALF, :])
 
         nc.sync.dma_start(bias[:], b.rearrange("(mb p) o -> p (mb o)", p=P))
 
@@ -60,16 +65,21 @@ def tile_scatter_matmul_kernel(tc, base, x, w, b, offs, out):
             window[(i, mb)] = windows.tile([P, TOKENS], F32, name="window_%d_%d" % (i, mb))
             nc.tensor.matmul(window[(i, mb)][:], ident[:], base_sb[i][:, mb, :], start=True, stop=False)
 
-        for n, (i, mb) in enumerate(blocks):
-            piece = offsets[:, i * PIECE_COLS : (i + 1) * PIECE_COLS]
-            for kb in range(K_BLOCKS):
+        def scattered(i, mb, kbs):
+            for kb in kbs:
                 nc.tensor.matmul(
-                    window[(i, mb)][:].indirect(piece),
-                    w_sb[:, kb, mb * P : (mb + 1) * P],
-                    x_sb[:, kb, i * PIECE : (i + 1) * PIECE],
+                    window[(i, mb)][:].indirect(offsets[:, i * PIECE_COLS : (i + 1) * PIECE_COLS]),
+                    w_sb[kb // K_HALF][:, kb % K_HALF, mb * P : (mb + 1) * P],
+                    x_sb[kb // K_HALF][:, kb % K_HALF, i * PIECE : (i + 1) * PIECE],
                     start=False,
                     stop=(kb == K_BLOCKS - 1),
                 )
+
+        for mb in range(M_BLOCKS):
+            scattered(0, mb, range(K_HALF))
+
+        for n, (i, mb) in enumerate(blocks):
+            scattered(i, mb, range(K_HALF if i == 0 else 0, K_BLOCKS))
             result = held.tile([P, TOKENS], F32, name="result_%d_%d" % (i, mb))
             for lo in (0, HALF):
                 nc.vector.tensor_scalar(

@@ -15,6 +15,7 @@ K_HALF = K_BLOCKS // 2
 M_BLOCKS = M // P
 PIECE_COLS = PIECE // 16
 HALF = TOKENS // 2
+SQUARE = 32
 WARM_COLS = 256
 WARM_UP = 6
 
@@ -32,12 +33,20 @@ def tile_scatter_matmul_kernel(tc, base, x, w, b, offs, out):
 
         blocks = [(i, mb) for i in range(SEQS) for mb in range(M_BLOCKS)]
 
-        bias = held.tile([P, M_BLOCKS], F32, name="bias")
+        bias_rows = held.tile([P, P], F32, name="bias_rows", align_bytes=64)
+        nc.gpsimd.memset(bias_rows[:], 0.0)
 
         base_sb = {}
         for i in range(SEQS):
             base_sb[i] = held.tile([P, M_BLOCKS, TOKENS], BF16, name="base_%d" % i)
             nc.sync.dma_start(base_sb[i][:], base[i].rearrange("(mb p) t -> p mb t", p=P))
+
+        nc.sync.dma_start(
+            bias_rows[0:P:SQUARE, 0 : M_BLOCKS * SQUARE].rearrange("q (mb r) -> q mb r", r=SQUARE),
+            b.rearrange("(mb q r) o -> q mb (r o)", mb=M_BLOCKS, r=SQUARE),
+        )
+        bias_cols = held.tile([P, P], F32, name="bias_cols", align_bytes=64)
+        nc.vector.transpose(bias_cols[:], bias_rows[:])
 
         offsets = held.tile([P, N // 16], U16, name="offsets")
         nc.sync.dma_start(offsets[:], offs)
@@ -50,8 +59,6 @@ def tile_scatter_matmul_kernel(tc, base, x, w, b, offs, out):
             nc.sync.dma_start(w_sb[h][:], w_rows[:, h * K_HALF : (h + 1) * K_HALF, :])
             x_sb.append(held.tile([P, K_HALF, N], BF16, name="x_%d" % h))
             nc.sync.dma_start(x_sb[h][:], x_rows[:, h * K_HALF : (h + 1) * K_HALF, :])
-
-        nc.sync.dma_start(bias[:], b.rearrange("(mb p) o -> p (mb o)", p=P))
 
         unread = windows.tile([P, WARM_COLS], F32, name="unread")
         for n in range(WARM_UP):
@@ -85,7 +92,7 @@ def tile_scatter_matmul_kernel(tc, base, x, w, b, offs, out):
                 nc.vector.tensor_scalar(
                     result[:, lo : lo + HALF],
                     window[(i, mb)][:, lo : lo + HALF],
-                    bias[:, mb : mb + 1],
+                    bias_cols[:, mb * SQUARE : mb * SQUARE + 1],
                     None,
                     mybir.AluOpType.add,
                 )

@@ -33,6 +33,9 @@ def tile_scatter_matmul_kernel(tc, base, x, w, b, offs, out):
 
         blocks = [(i, mb) for i in range(SEQS) for mb in range(M_BLOCKS)]
 
+        early = held.tile([P, 1], F32, name="early")
+        nc.scalar.activation(early[:], zeros[:, 0:1], mybir.ActivationFunctionType.Identity)
+
         bias_rows = held.tile([P, P], F32, name="bias_rows", align_bytes=64)
         nc.gpsimd.memset(bias_rows[:], 0.0)
 
@@ -89,11 +92,19 @@ def tile_scatter_matmul_kernel(tc, base, x, w, b, offs, out):
             scattered(i, mb, range(K_HALF if i == 0 else 0, K_BLOCKS))
             result = held.tile([P, TOKENS], F32, name="result_%d_%d" % (i, mb))
             for lo in (0, HALF):
-                nc.vector.tensor_scalar(
-                    result[:, lo : lo + HALF],
-                    window[(i, mb)][:, lo : lo + HALF],
-                    bias_cols[:, mb * SQUARE : mb * SQUARE + 1],
-                    None,
-                    mybir.AluOpType.add,
-                )
+                if n % 2 == 0:
+                    nc.vector.tensor_scalar(
+                        result[:, lo : lo + HALF],
+                        window[(i, mb)][:, lo : lo + HALF],
+                        bias_cols[:, mb * SQUARE : mb * SQUARE + 1],
+                        None,
+                        mybir.AluOpType.add,
+                    )
+                else:
+                    nc.scalar.activation(
+                        result[:, lo : lo + HALF],
+                        window[(i, mb)][:, lo : lo + HALF],
+                        mybir.ActivationFunctionType.Identity,
+                        bias=bias_cols[:, mb * SQUARE : mb * SQUARE + 1],
+                    )
                 nc.sync.dma_start(out[i, mb * P : (mb + 1) * P, lo : lo + HALF], result[:, lo : lo + HALF])

import concourse.mybir as mybir
from concourse.masks import make_identity

BF16, F32, U16 = mybir.dt.bfloat16, mybir.dt.float32, mybir.dt.uint16

P = 128
SEQS = 2
TOKENS = 512
K = 512
M = 256
N = 192
PIECE = N // SEQS
K_BLOCKS = K // P
K_HALF = K_BLOCKS // 2
M_BLOCKS = M // P
PIECE_COLS = PIECE // 16
HALF = TOKENS // 2
SQUARE = 32
WARM_COLS = 256
WARM_UP = 6

FLOPS = 2 * K * M * N


def tile_scatter_matmul_kernel(tc, base, x, w, b, offs, out):
    nc = tc.nc
    with (
        tc.tile_pool(name="held", bufs=1) as held,
        tc.psum_pool(name="windows", bufs=1) as windows,
    ):
        zeros = held.tile([P, WARM_COLS], BF16, name="zeros")
        nc.gpsimd.memset(zeros[:], 0.0)

        blocks = [(i, mb) for i in range(SEQS) for mb in range(M_BLOCKS)]

        early = held.tile([P, 1], F32, name="early")
        nc.scalar.activation(early[:], zeros[:, 0:1], mybir.ActivationFunctionType.Identity)

        bias_rows = held.tile([P, P], F32, name="bias_rows", align_bytes=64)
        nc.gpsimd.memset(bias_rows[:], 0.0)

        base_sb = {}
        for i in range(SEQS):
            base_sb[i] = held.tile([P, M_BLOCKS, TOKENS], BF16, name="base_%d" % i)
            nc.sync.dma_start(base_sb[i][:], base[i].rearrange("(mb p) t -> p mb t", p=P))

        nc.sync.dma_start(
            bias_rows[0:P:SQUARE, 0 : M_BLOCKS * SQUARE].rearrange("q (mb r) -> q mb r", r=SQUARE),
            b.rearrange("(mb q r) o -> q mb (r o)", mb=M_BLOCKS, r=SQUARE),
        )
        bias_cols = held.tile([P, P], F32, name="bias_cols", align_bytes=64)
        nc.vector.transpose(bias_cols[:], bias_rows[:])

        offsets = held.tile([P, N // 16], U16, name="offsets")
        nc.sync.dma_start(offsets[:], offs)

        w_rows = w.rearrange("(p kb) m -> p kb m", p=P)
        x_rows = x.rearrange("(p kb) n -> p kb n", p=P)
        w_sb, x_sb = [], []
        for h in range(K_BLOCKS // K_HALF):
            w_sb.append(held.tile([P, K_HALF, M], BF16, name="w_%d" % h))
            nc.sync.dma_start(w_sb[h][:], w_rows[:, h * K_HALF : (h + 1) * K_HALF, :])
            x_sb.append(held.tile([P, K_HALF, N], BF16, name="x_%d" % h))
            nc.sync.dma_start(x_sb[h][:], x_rows[:, h * K_HALF : (h + 1) * K_HALF, :])

        unread = windows.tile([P, WARM_COLS], F32, name="unread")
        for n in range(WARM_UP):
            nc.tensor.matmul(unread[:], zeros[:, 0:P], zeros[:], start=True, stop=True)

        ident = held.tile([P, P], BF16, name="ident")
        make_identity(nc, ident[:])

        window = {}
        for i, mb in blocks:
            window[(i, mb)] = windows.tile([P, TOKENS], F32, name="window_%d_%d" % (i, mb))
            nc.tensor.matmul(window[(i, mb)][:], ident[:], base_sb[i][:, mb, :], start=True, stop=False)

        def scattered(i, mb, kbs):
            for kb in kbs:
                nc.tensor.matmul(
                    window[(i, mb)][:].indirect(offsets[:, i * PIECE_COLS : (i + 1) * PIECE_COLS]),
                    w_sb[kb // K_HALF][:, kb % K_HALF, mb * P : (mb + 1) * P],
                    x_sb[kb // K_HALF][:, kb % K_HALF, i * PIECE : (i + 1) * PIECE],
                    start=False,
                    stop=(kb == K_BLOCKS - 1),
                )

        for mb in range(M_BLOCKS):
            scattered(0, mb, range(K_HALF))

        for n, (i, mb) in enumerate(blocks):
            scattered(i, mb, range(K_HALF if i == 0 else 0, K_BLOCKS))
            result = held.tile([P, TOKENS], F32, name="result_%d_%d" % (i, mb))
            for lo in (0, HALF):
                if n % 2 == 0:
                    nc.vector.tensor_scalar(
                        result[:, lo : lo + HALF],
                        window[(i, mb)][:, lo : lo + HALF],
                        bias_cols[:, mb * SQUARE : mb * SQUARE + 1],
                        None,
                        mybir.AluOpType.add,
                    )
                else:
                    nc.scalar.activation(
                        result[:, lo : lo + HALF],
                        window[(i, mb)][:, lo : lo + HALF],
                        mybir.ActivationFunctionType.Identity,
                        bias=bias_cols[:, mb * SQUARE : mb * SQUARE + 1],
                    )
                nc.sync.dma_start(out[i, mb * P : (mb + 1) * P, lo : lo + HALF], result[:, lo : lo + HALF])
